import numpy as np
import ml_dtypes


def mxq(x, axis, fmt="e4m3"):
    dtype, down = {"e4m3": (ml_dtypes.float8_e4m3fn, 7), "e5m2": (ml_dtypes.float8_e5m2, 14)}[fmt]
    v = np.moveaxis(np.asarray(x, np.float32).astype(ml_dtypes.bfloat16).astype(np.float64), axis, -1)
    blocks = v.reshape(v.shape[:-1] + (-1, 32))
    amax = np.abs(blocks).max(-1, keepdims=True)
    byte = np.maximum(np.where(amax > 0, np.frexp(amax)[1] - 1 + 127, 0) - down, 1)
    scale = np.exp2(byte - 127.0)
    codes = (blocks / scale).astype(np.float32).astype(dtype).astype(np.float64)
    return np.moveaxis((codes * scale).reshape(v.shape), -1, axis)


WIDE = False


def mx_kscale(k):
    if not WIDE:
        return np.ones(k)
    levels = np.array([10, -10, 5, -5, 0])
    if k % 512:
        return np.exp2(np.random.permutation(np.resize(levels, k // 32))).repeat(32)
    a = np.empty((k // 512, 16))
    for p in range(k // 512):
        a[p, :8] = np.random.permutation(np.resize(levels, 8))
        for g in range(8):
            far = levels[np.abs(levels - a[p, g]) >= 10]
            a[p, g + 8] = far[np.random.randint(len(far))]
    return np.exp2(a.ravel()).repeat(32)


def f64(x):
    return np.asarray(x).astype(np.float64)


def striped(idx):
    return np.tile(np.asarray(idx).reshape(-1, 16).T, (8, 1)).astype(np.uint16)


def unstriped(offs):
    return offs[:16].T.reshape(-1).astype(np.int64)


E2M1 = np.array([0.0, 0.5, 1.0, 1.5, 2.0, 3.0, 4.0, 6.0, -0.0, -0.5, -1.0, -1.5, -2.0, -3.0, -4.0, -6.0])


def pack_weight(w, fmt):
    k, n = w.shape
    w = f64(np.asarray(w, np.float32).astype(ml_dtypes.bfloat16)).reshape(k // 32, 32, n)
    amax = np.abs(w).max(1)
    if fmt == "e4m3":
        byte = np.frexp(amax)[1] - 1 + 127 - 7
    else:
        mant, ex = np.frexp(amax / 6.0)
        byte = np.where(mant > 0.5, ex, ex - 1) + 127
    byte = np.clip(np.where(amax > 0, byte, 1), 1, 254)
    scaled = (w * np.exp2(127.0 - byte)[:, None, :]).reshape(k, n).astype(np.float32)
    by_word = np.ascontiguousarray(scaled.reshape(k // 512, 128, 4, n).transpose(0, 1, 3, 2))
    if fmt == "e4m3":
        words = by_word.astype(ml_dtypes.float8_e4m3fn).view(np.uint8)
    else:
        c = by_word.astype(ml_dtypes.float4_e2m1fn).view(np.uint8) & 0xF
        words = (c[..., 0::2] | (c[..., 1::2] << 4)).reshape(k // 512, 128, 2 * n)
    return np.ascontiguousarray(words), np.ascontiguousarray(byte.astype(np.uint8).reshape(k // 512, 16, n))


def unpack_weight(words, scales, fmt):
    g, _, n = scales.shape
    words = np.ascontiguousarray(words).reshape(g, 128, n, -1)
    if fmt == "e4m3":
        vals = words.view(ml_dtypes.float8_e4m3fn).astype(np.float64)
    else:
        nib = np.empty((g, 128, n, 4), np.uint8)
        nib[..., 0::2] = words & 0xF
        nib[..., 1::2] = words >> 4
        vals = E2M1[nib]
    vals = vals * np.repeat(np.exp2(scales.astype(np.float64) - 127.0), 8, axis=1)[..., None]
    return vals.transpose(0, 1, 3, 2).reshape(g * 512, n)


D, E, T, I, Q, G = 512, 512, 2048, 512, 256, 32


def setup_inputs():
    n = np.random.standard_normal
    idx = np.random.permutation(T)[:I]
    fd = mx_kscale(D)
    fe = mx_kscale(E)
    keysp = pack_weight(n((D, T)) / fd[:, None], "e4m3")
    valsp = pack_weight(n((E, T)) / fe[:, None], "e4m3")
    return {
        "query": (n((D, Q)) * 0.7 / np.sqrt(D) * fd[:, None]).astype(np.float32),
        "keys_words": keysp[0],
        "keys_scales": keysp[1],
        "reserve": (np.random.uniform(1.0, 8.0, (I, 1))).astype(np.float32),
        "us": (np.random.uniform(0.5, 2.0, (I, 1))).astype(np.float32),
        "gout": (n((E, Q)) * 1 / np.sqrt(E) * fe[:, None]).astype(np.float32),
        "vals_words": valsp[0],
        "vals_scales": valsp[1],
        "dquery": (n((D, Q)) * 1.0 / np.sqrt(D) * fd[:, None]).astype(np.float32),
        "base": (0.5 * n((I, Q))).astype(np.float32),
        "offs": striped(idx),
    }


def reference(query, keys_words, keys_scales, reserve, us, gout, vals_words, vals_scales, dquery, base, offs):
    idx = unstriped(offs)
    keysu = unpack_weight(keys_words, keys_scales, "e4m3")
    valsu = unpack_weight(vals_words, vals_scales, "e4m3")
    keysidxg = keysu[:, idx]
    queryq = mxq(f64(query), 0, "e4m3")
    a = keysidxg.T @ queryq
    dqueryq = mxq(f64(dquery), 0, "e4m3")
    ta = keysidxg.T @ dqueryq
    p = np.exp(a)
    b = f64(us) / (p.reshape(I, G, Q // G).sum(axis=2) + f64(reserve))
    br = np.repeat(b, Q // G, axis=1)
    valsidxg = valsu[:, idx]
    goutq = mxq(f64(gout), 0, "e4m3")
    c0 = valsidxg.T @ goutq
    dbr = c0 * p
    db = dbr.reshape(I, G, Q // G).sum(axis=2)
    e1 = db * f64(us) / np.square(p.reshape(I, G, Q // G).sum(axis=2) + f64(reserve)) * (-1.0)
    r1 = np.repeat(e1, Q // G, axis=1)
    dp = c0 * br + r1
    tp = ta * p
    tb = tp.reshape(I, G, Q // G).sum(axis=2) * f64(us) / np.square(p.reshape(I, G, Q // G).sum(axis=2) + f64(reserve)) * (-1.0)
    tbr = np.repeat(tb, Q // G, axis=1)
    tdbr = tp * c0
    tdb = tdbr.reshape(I, G, Q // G).sum(axis=2)
    te1 = (tdb * f64(us) - tp.reshape(I, G, Q // G).sum(axis=2) * (p.reshape(I, G, Q // G).sum(axis=2) + f64(reserve)) * 2.0 * db * f64(us) / np.square(p.reshape(I, G, Q // G).sum(axis=2) + f64(reserve))) / np.square(p.reshape(I, G, Q // G).sum(axis=2) + f64(reserve)) * (-1.0)
    tr1 = np.repeat(te1, Q // G, axis=1)
    tdp = tbr * c0 + tr1
    tda = tdp * p + tp * dp
    y = tda * 8.0 + f64(base)
    return y

@@ -1,0 +1,233 @@
+from contextlib import ExitStack
+
+import concourse.mybir as mybir
+from concourse.masks import make_identity
+
+D, E, T, I, Q, G = 512, 512, 2048, 512, 256, 32
+FLOPS = 2 * I * Q * (D + D + E)
+
+F32 = mybir.dt.float32
+BF16 = mybir.dt.bfloat16
+I32 = mybir.dt.int32
+U32 = mybir.dt.uint32
+U16 = mybir.dt.uint16
+U8 = mybir.dt.uint8
+FP8X4 = mybir.dt.float8_e4m3fn_x4
+ALU = mybir.AluOpType
+ACT = mybir.ActivationFunctionType
+AXIS_X = mybir.AxisListType.X
+
+P = 128
+PACK = 4
+TEAM = Q // G
+TILES = I // P
+HALVES = 2
+PER_HALF = TILES // HALVES
+HALF_SLOTS = I // HALVES
+HALF_COLS = PER_HALF * Q
+HALF_TEAMS = PER_HALF * G
+OUT_FACTOR = 8.0
+
+
+def tile_attend_hvteamshares_d_kernel(tc, query, keys_words, keys_scales, reserve, us, gout, vals_words, vals_scales, dquery, base, offs, out):
+    nc = tc.nc
+    with ExitStack() as ctx:
+        held = ctx.enter_context(tc.tile_pool(name="held", bufs=1))
+        stage = ctx.enter_context(tc.tile_pool(name="stage", bufs=2))
+        psum = ctx.enter_context(tc.psum_pool(name="psum", bufs=1))
+
+        def sb(name, shape, dtype=F32):
+            return held.tile(shape, dtype, name=name, align_bytes=64)
+
+        def teams(ap):
+            return ap.rearrange("p (n j) -> p n j", j=TEAM)
+
+        def spread(ap):
+            return ap.unsqueeze(2).to_broadcast([P, ap.shape[1], TEAM])
+
+        def load_scale_rows(queue, window, scales, quadrant):
+            queue.dma_start(
+                out=window[32 * quadrant : 32 * quadrant + 4, :].bitcast(I32),
+                in_=scales[0, 4 * quadrant : 4 * quadrant + 4, :].bitcast(I32),
+            )
+
+        def load_rows(src, name):
+            raw = stage.tile([P, PACK, Q], F32, name=name, tag="raw", align_bytes=64)
+            nc.sync.dma_start(out=raw[:], in_=src.rearrange("(p t) q -> p t q", t=PACK))
+            return raw
+
+        def round_and_interleave(raw, name):
+            grouped = sb(name, [P, Q, PACK], BF16)
+            nc.scalar.activation(
+                out=grouped[:].rearrange("p (c i) t -> p c t i", i=4),
+                in_=raw[:].rearrange("p t (c i) -> p c t i", i=4),
+                func=ACT.Copy,
+            )
+            return grouped
+
+        def quantize(grouped, name):
+            codes = sb(name + "_codes", [P, Q], U32)
+            plane = sb(name + "_plane", [P, Q], U8)
+            nc.vector.quantize_mx(out=codes[:].bitcast(FP8X4), scales=plane[:], in_=grouped[:].rearrange("p q t -> p (q t)"))
+            return codes, plane
+
+        def products(bank, words, scale_bytes, h, moving):
+            codes, plane = moving
+            for s in range(PER_HALF):
+                slot0 = HALF_SLOTS * h + P * s
+                nc.tensor.matmul_mx(
+                    out=bank[:, Q * s : Q * (s + 1)],
+                    lhsT=words[:, P * s : P * (s + 1)].bitcast(FP8X4),
+                    lhsT_scale=scale_bytes[:, slot0 : slot0 + P],
+                    rhs=codes[:].bitcast(FP8X4),
+                    rhs_scale=plane[:],
+                    start=True,
+                    stop=True,
+                )
+
+        offsets = held.tile([P, I // 16], U16, name="offsets")
+        key_scale_pool = sb("key_scale_pool", [P, T], U8)
+        val_scale_pool = sb("val_scale_pool", [P, T], U8)
+        key_pool = sb("key_pool", [P, T], I32)
+        val_pool = sb("val_pool", [P, T], I32)
+
+        nc.gpsimd.memset(key_scale_pool[:].bitcast(I32), 0)
+        nc.vector.memset(val_scale_pool[:].bitcast(I32), 0)
+        nc.sync.dma_start(offsets[:], offs)
+        query_raw = load_rows(query, "query_raw")
+        for quadrant in range(4):
+            load_scale_rows(nc.sync, key_scale_pool, keys_scales, quadrant)
+        nc.sync.dma_start(out=key_pool[:], in_=keys_words[0].rearrange("p n t -> p (n t)").bitcast(I32))
+        dquery_raw = load_rows(dquery, "dquery_raw")
+        for quadrant in range(4):
+            load_scale_rows(nc.scalar, val_scale_pool, vals_scales, quadrant)
+        nc.sync.dma_start(out=val_pool[:], in_=vals_words[0].rearrange("p n t -> p (n t)").bitcast(I32))
+
+        slot_rows = sb("slot_rows", [P, P])
+        identity = sb("identity", [P, P])
+        nc.gpsimd.memset(slot_rows[:], 0.0)
+        nc.gpsimd.dma_start(out=slot_rows[0:TILES, :], in_=reserve.rearrange("(r p) o -> r (p o)", p=P))
+        nc.gpsimd.dma_start(out=slot_rows[TILES : 2 * TILES, :], in_=us.rearrange("(r p) o -> r (p o)", p=P))
+        make_identity(nc, identity[:])
+        slot_cols_ps = psum.tile([P, P], F32, name="slot_cols_ps")
+        nc.tensor.transpose(slot_cols_ps[:], slot_rows[:], identity[:])
+
+        key_scales = sb("key_scales", [P, I], U8)
+        nc.vector.tensor_copy(key_scales[:], key_scale_pool[:].indirect(offsets[:]))
+        query_mx = quantize(round_and_interleave(query_raw, "query_bf"), "query")
+        val_scales = sb("val_scales", [P, I], U8)
+        nc.vector.tensor_copy(val_scales[:], val_scale_pool[:].indirect(offsets[:]))
+
+        def gather_words(pool_tile, h, name):
+            words = sb(name, [P, HALF_SLOTS], U32)
+            cols = HALF_SLOTS // 16
+            nc.vector.tensor_copy(words[:], pool_tile[:].bitcast(U32).indirect(offsets[:, cols * h : cols * (h + 1)]))
+            return words
+
+        key_words, p = [], []
+        for h in range(HALVES):
+            key_words.append(gather_words(key_pool, h, "key_words%d" % h))
+            a_ps = psum.tile([P, HALF_COLS], F32, name="a_ps%d" % h)
+            products(a_ps, key_words[h], key_scales, h, query_mx)
+            p.append(sb("p%d" % h, [P, HALF_COLS]))
+            nc.scalar.activation(out=p[h][:], in_=a_ps[:], func=ACT.Exp)
+
+        res = sb("res", [P, TILES])
+        u8 = sb("u8", [P, TILES])
+        nc.scalar.activation(out=res[:], in_=slot_cols_ps[:, 0:TILES], func=ACT.Copy)
+        nc.scalar.activation(out=u8[:], in_=slot_cols_ps[:, TILES : 2 * TILES], func=ACT.Copy, scale=OUT_FACTOR)
+
+        dquery_bf = round_and_interleave(dquery_raw, "dquery_bf")
+        gout_raw = load_rows(gout, "gout_raw")
+
+        def res_of(h):
+            return res[:, PER_HALF * h : PER_HALF * (h + 1)].unsqueeze(2).to_broadcast([P, PER_HALF, G])
+
+        def by_tile(ap):
+            return ap.rearrange("p (s g) -> p s g", g=G)
+
+        rinv, pn = [], []
+        sums = []
+        for h in range(HALVES):
+            sums.append(sb("psum_team%d" % h, [P, HALF_TEAMS]))
+            nc.vector.tensor_reduce(out=sums[h][:], in_=teams(p[h][:]), axis=AXIS_X, op=ALU.add)
+        dquery_mx = quantize(dquery_bf, "dquery")
+        for h in range(HALVES):
+            denom = sb("denom%d" % h, [P, HALF_TEAMS])
+            nc.vector.tensor_tensor(out=by_tile(denom[:]), in0=by_tile(sums[h][:]), in1=res_of(h), op=ALU.add)
+            rinv.append(sb("rinv%d" % h, [P, HALF_TEAMS]))
+            nc.vector.reciprocal(out=rinv[h][:], in_=denom[:])
+            pn.append(sb("pn%d" % h, [P, HALF_COLS]))
+            nc.gpsimd.tensor_tensor(out=teams(pn[h][:]), in0=teams(p[h][:]), in1=spread(rinv[h][:]), op=ALU.mult)
+
+        ta_ps = []
+        for h in range(HALVES):
+            ta_ps.append(psum.tile([P, HALF_COLS], F32, name="ta_ps%d" % h))
+            products(ta_ps[h], key_words[h], key_scales, h, dquery_mx)
+
+        gout_bf = round_and_interleave(gout_raw, "gout_bf")
+        base_sb = stage.tile([P, TILES, Q], F32, name="base_sb", tag="raw", align_bytes=64)
+        nc.sync.dma_start(out=base_sb[:], in_=base.rearrange("(r p) q -> p r q", p=P))
+
+        tp, tsum = [], []
+        for h in range(HALVES):
+            tp.append(sb("tp%d" % h, [P, HALF_COLS]))
+            nc.vector.tensor_tensor(out=tp[h][:], in0=ta_ps[h][:], in1=p[h][:], op=ALU.mult)
+        for h in range(HALVES):
+            tsum.append(sb("tsum%d" % h, [P, HALF_TEAMS]))
+            nc.vector.tensor_reduce(out=tsum[h][:], in_=teams(tp[h][:]), axis=AXIS_X, op=ALU.add)
+        val_words = [gather_words(val_pool, h, "val_words%d" % h) for h in range(HALVES)]
+        tmean, x, z = [], [], []
+        for h in range(HALVES):
+            tmean.append(sb("tmean%d" % h, [P, HALF_TEAMS]))
+            nc.vector.tensor_tensor(out=tmean[h][:], in0=tsum[h][:], in1=rinv[h][:], op=ALU.mult)
+        for h in range(HALVES):
+            f = sb("f%d" % h, [P, HALF_COLS])
+            nc.vector.tensor_tensor(out=teams(f[:]), in0=teams(ta_ps[h][:]), in1=spread(tmean[h][:]), op=ALU.subtract)
+            x.append(sb("x%d" % h, [P, HALF_COLS]))
+            nc.gpsimd.tensor_tensor(out=x[h][:], in0=f[:], in1=pn[h][:], op=ALU.mult)
+        gout_mx = quantize(gout_bf, "gout")
+        for h in range(HALVES):
+            rho = sb("rho%d" % h, [P, HALF_TEAMS])
+            nc.vector.tensor_tensor(out=by_tile(rho[:]), in0=by_tile(rinv[h][:]), in1=res_of(h), op=ALU.mult)
+            z.append(sb("z%d" % h, [P, HALF_TEAMS]))
+            nc.vector.tensor_tensor(out=z[h][:], in0=rho[:], in1=tmean[h][:], op=ALU.mult)
+
+        c_ps = []
+        for h in range(HALVES):
+            c_ps.append(psum.tile([P, HALF_COLS], F32, name="c_ps%d" % h))
+            products(c_ps[h], val_words[h], val_scales, h, gout_mx)
+
+        def c_of(r):
+            return c_ps[r // PER_HALF][:, Q * (r % PER_HALF) : Q * (r % PER_HALF + 1)]
+
+        def cols_of(tiles, r, width):
+            return tiles[r // PER_HALF][:, width * (r % PER_HALF) : width * (r % PER_HALF + 1)]
+
+        pc = [sb("pc%d" % h, [P, HALF_COLS]) for h in range(HALVES)]
+        m8 = [sb("m8_%d" % h, [P, HALF_TEAMS]) for h in range(HALVES)]
+        g8 = [sb("g8_%d" % r, [P, Q]) for r in range(TILES)]
+        y = [sb("y%d" % r, [P, Q]) for r in range(TILES)]
+        yb = [sb("yb%d" % r, [P, Q]) for r in range(TILES)]
+        mz = [sb("mz%d" % h, [P, HALF_TEAMS]) for h in range(HALVES)]
+        for h in range(HALVES):
+            for r in range(PER_HALF * h, PER_HALF * (h + 1)):
+                nc.vector.scalar_tensor_tensor(out=cols_of(pc, r, Q), in0=c_of(r), scalar=u8[:, r : r + 1], in1=cols_of(pn, r, Q), op0=ALU.mult, op1=ALU.mult)
+            nc.vector.tensor_reduce(out=m8[h][:], in_=teams(pc[h][:]), axis=AXIS_X, op=ALU.add)
+        for h in range(HALVES):
+            for r in range(PER_HALF * h, PER_HALF * (h + 1)):
+                nc.vector.scalar_tensor_tensor(out=teams(g8[r][:]), in0=teams(c_of(r)), scalar=u8[:, r : r + 1], in1=spread(cols_of(m8, r, G)), op0=ALU.mult, op1=ALU.subtract)
+                nc.gpsimd.tensor_tensor(out=y[r][:], in0=g8[r][:], in1=cols_of(x, r, Q), op=ALU.mult)
+            nc.vector.tensor_tensor(out=mz[h][:], in0=m8[h][:], in1=z[h][:], op=ALU.mult)
+        for r in range(TILES):
+            nc.gpsimd.tensor_tensor(out=yb[r][:], in0=y[r][:], in1=base_sb[:, r, :], op=ALU.add)
+        for r in range(TILES):
+            ysum = sb("ysum%d" % r, [P, G])
+            nc.vector.tensor_reduce(out=ysum[:], in_=teams(y[r][:]), axis=AXIS_X, op=ALU.add)
+            kappa = sb("kappa%d" % r, [P, G])
+            nc.vector.tensor_tensor(out=kappa[:], in0=ysum[:], in1=cols_of(mz, r, G), op=ALU.add)
+            kp = sb("kp%d" % r, [P, Q])
+            nc.vector.tensor_tensor(out=teams(kp[:]), in0=teams(cols_of(pn, r, Q)), in1=spread(kappa[:]), op=ALU.mult)
+            res_tile = sb("result%d" % r, [P, Q])
+            nc.vector.tensor_tensor(out=res_tile[:], in0=yb[r][:], in1=kp[:], op=ALU.subtract)
+            nc.sync.dma_start(out=out[P * r : P * (r + 1), :], in_=res_tile[:])

@@ -33,7 +33,7 @@ def tile_attend_hvteamshares_d_kernel(tc, query, keys_words, keys_scales, reserv
     nc = tc.nc
     with ExitStack() as ctx:
         held = ctx.enter_context(tc.tile_pool(name="held", bufs=1))
-        stage = ctx.enter_context(tc.tile_pool(name="stage", bufs=2))
+        stage = ctx.enter_context(tc.tile_pool(name="stage", bufs=1))
         psum = ctx.enter_context(tc.psum_pool(name="psum", bufs=1))
 
         def sb(name, shape, dtype=F32):
@@ -51,18 +51,24 @@ def tile_attend_hvteamshares_d_kernel(tc, query, keys_words, keys_scales, reserv
                 in_=scales[0, 4 * quadrant : 4 * quadrant + 4, :].bitcast(I32),
             )
 
-        def load_rows(src, name):
-            raw = stage.tile([P, PACK, Q], F32, name=name, tag="raw", align_bytes=64)
+        def staged(name, shape, dtype, tag):
+            return stage.tile(shape, dtype, name=name, tag=tag, align_bytes=64)
+
+        def load_rows(src, name, tag):
+            raw = staged(name, [P, PACK, Q], F32, tag)
             nc.sync.dma_start(out=raw[:], in_=src.rearrange("(p t) q -> p t q", t=PACK))
             return raw
 
-        def round_and_interleave(raw, name):
+        def round_and_interleave(raw, name, pieces=1):
             grouped = sb(name, [P, Q, PACK], BF16)
-            nc.scalar.activation(
-                out=grouped[:].rearrange("p (c i) t -> p c t i", i=4),
-                in_=raw[:].rearrange("p t (c i) -> p c t i", i=4),
-                func=ACT.Copy,
-            )
+            width = Q // pieces
+            for piece in range(pieces):
+                cols = slice(width * piece, width * (piece + 1))
+                nc.scalar.activation(
+                    out=grouped[:, cols, :].rearrange("p (c i) t -> p c t i", i=4),
+                    in_=raw[:, :, cols].rearrange("p t (c i) -> p c t i", i=4),
+                    func=ACT.Copy,
+                )
             return grouped
 
         def quantize(grouped, name):
@@ -88,20 +94,18 @@ def tile_attend_hvteamshares_d_kernel(tc, query, keys_words, keys_scales, reserv
         offsets = held.tile([P, I // 16], U16, name="offsets")
         key_scale_pool = sb("key_scale_pool", [P, T], U8)
         val_scale_pool = sb("val_scale_pool", [P, T], U8)
-        key_pool = sb("key_pool", [P, T], I32)
-        val_pool = sb("val_pool", [P, T], I32)
+        key_pool = staged("key_pool", [P, T], I32, "c")
 
         nc.gpsimd.memset(key_scale_pool[:].bitcast(I32), 0)
         nc.vector.memset(val_scale_pool[:].bitcast(I32), 0)
-        nc.sync.dma_start(offsets[:], offs)
-        query_raw = load_rows(query, "query_raw")
         for quadrant in range(4):
             load_scale_rows(nc.sync, key_scale_pool, keys_scales, quadrant)
+        nc.sync.dma_start(offsets[:], offs)
+        query_raw = load_rows(query, "query_raw", "a")
+        dquery_raw = load_rows(dquery, "dquery_raw", "b")
         nc.sync.dma_start(out=key_pool[:], in_=keys_words[0].rearrange("p n t -> p (n t)").bitcast(I32))
-        dquery_raw = load_rows(dquery, "dquery_raw")
         for quadrant in range(4):
-            load_scale_rows(nc.scalar, val_scale_pool, vals_scales, quadrant)
-        nc.sync.dma_start(out=val_pool[:], in_=vals_words[0].rearrange("p n t -> p (n t)").bitcast(I32))
+            load_scale_rows(nc.sync, val_scale_pool, vals_scales, quadrant)
 
         slot_rows = sb("slot_rows", [P, P])
         identity = sb("identity", [P, P])
@@ -109,125 +113,126 @@ def tile_attend_hvteamshares_d_kernel(tc, query, keys_words, keys_scales, reserv
         nc.gpsimd.dma_start(out=slot_rows[0:TILES, :], in_=reserve.rearrange("(r p) o -> r (p o)", p=P))
         nc.gpsimd.dma_start(out=slot_rows[TILES : 2 * TILES, :], in_=us.rearrange("(r p) o -> r (p o)", p=P))
         make_identity(nc, identity[:])
-        slot_cols_ps = psum.tile([P, P], F32, name="slot_cols_ps")
+
+        first = [held.tile([P, TEAM + 1, 2 * HALF_TEAMS], F32, name="first%d" % h, tag="first%d" % h, align_bytes=64) for h in range(HALVES)]
+        second = [sb("second%d" % h, [P, TEAM, 2 * HALF_TEAMS]) for h in range(HALVES)]
+        for h in range(HALVES):
+            nc.gpsimd.memset(first[h][:, TEAM, HALF_TEAMS:], 0.0)
+
+        slot_cols_ps = psum.tile([P, P], F32, name="slot_cols_ps", tag="turned", bufs=2)
         nc.tensor.transpose(slot_cols_ps[:], slot_rows[:], identity[:])
 
         key_scales = sb("key_scales", [P, I], U8)
         nc.vector.tensor_copy(key_scales[:], key_scale_pool[:].indirect(offsets[:]))
         query_mx = quantize(round_and_interleave(query_raw, "query_bf"), "query")
-        val_scales = sb("val_scales", [P, I], U8)
-        nc.vector.tensor_copy(val_scales[:], val_scale_pool[:].indirect(offsets[:]))
+        dquery_mx = quantize(round_and_interleave(dquery_raw, "dquery_bf"), "dquery")
+        val_pool = staged("val_pool", [P, T], I32, "a")
+        nc.sync.dma_start(out=val_pool[:], in_=vals_words[0].rearrange("p n t -> p (n t)").bitcast(I32))
+
+        gout_raw = load_rows(gout, "gout_raw", "b")
+
+        u8 = sb("u8", [P, TILES])
+        nc.scalar.activation(out=u8[:], in_=slot_cols_ps[:, TILES : 2 * TILES], func=ACT.Copy, scale=OUT_FACTOR)
+        for h in range(HALVES):
+            nc.scalar.activation(
+                out=first[h][:, TEAM, 0:HALF_TEAMS].rearrange("p (s g) -> p s g", g=G),
+                in_=slot_cols_ps[:, PER_HALF * h : PER_HALF * (h + 1)].unsqueeze(2).to_broadcast([P, PER_HALF, G]),
+                func=ACT.Copy,
+            )
 
         def gather_words(pool_tile, h, name):
-            words = sb(name, [P, HALF_SLOTS], U32)
+            words = staged(name, [P, HALF_SLOTS], U32, name)
             cols = HALF_SLOTS // 16
             nc.vector.tensor_copy(words[:], pool_tile[:].bitcast(U32).indirect(offsets[:, cols * h : cols * (h + 1)]))
             return words
 
-        key_words, p = [], []
+        def members(ap):
+            return ap.rearrange("p (n j) -> p j n", j=TEAM)
+
+        def team_sums(rows, name, tag, turned_sb):
+            bank = psum.tile([P, 2, P], F32, name=name + "_bank", tag=tag, bufs=2)
+            turned, sums = bank[:, 0, :], bank[:, 1, :]
+            count = rows.shape[1]
+            for j in range(count):
+                nc.tensor.matmul(turned, lhsT=rows[:, j, :], rhs=identity[:], start=(j == 0), stop=(j == count - 1), is_transpose=True)
+            nc.scalar.copy(out=turned_sb, in_=turned)
+            nc.tensor.transpose(sums, turned_sb, identity[:])
+            return sums
+
+        key_words = [gather_words(key_pool, h, "key_words%d" % h) for h in range(HALVES)]
+        val_scales = sb("val_scales", [P, I], U8)
+        nc.vector.tensor_copy(val_scales[:], val_scale_pool[:].indirect(offsets[:]))
+
+        a_ps, ta_ps, p = [], [], []
         for h in range(HALVES):
-            key_words.append(gather_words(key_pool, h, "key_words%d" % h))
-            a_ps = psum.tile([P, HALF_COLS], F32, name="a_ps%d" % h)
-            products(a_ps, key_words[h], key_scales, h, query_mx)
-            p.append(sb("p%d" % h, [P, HALF_COLS]))
-            nc.scalar.activation(out=p[h][:], in_=a_ps[:], func=ACT.Exp)
-
-        res = sb("res", [P, TILES])
-        u8 = sb("u8", [P, TILES])
-        nc.scalar.activation(out=res[:], in_=slot_cols_ps[:, 0:TILES], func=ACT.Copy)
-        nc.scalar.activation(out=u8[:], in_=slot_cols_ps[:, TILES : 2 * TILES], func=ACT.Copy, scale=OUT_FACTOR)
-
-        dquery_bf = round_and_interleave(dquery_raw, "dquery_bf")
-        gout_raw = load_rows(gout, "gout_raw")
-
-        def res_of(h):
-            return res[:, PER_HALF * h : PER_HALF * (h + 1)].unsqueeze(2).to_broadcast([P, PER_HALF, G])
-
-        def by_tile(ap):
-            return ap.rearrange("p (s g) -> p s g", g=G)
-
-        rinv, pn = [], []
-        sums = []
-        for h in range(HALVES):
-            sums.append(sb("psum_team%d" % h, [P, HALF_TEAMS]))
-            nc.vector.tensor_reduce(out=sums[h][:], in_=teams(p[h][:]), axis=AXIS_X, op=ALU.add)
-        dquery_mx = quantize(dquery_bf, "dquery")
-        for h in range(HALVES):
-            denom = sb("denom%d" % h, [P, HALF_TEAMS])
-            nc.vector.tensor_tensor(out=by_tile(denom[:]), in0=by_tile(sums[h][:]), in1=res_of(h), op=ALU.add)
-            rinv.append(sb("rinv%d" % h, [P, HALF_TEAMS]))
-            nc.vector.reciprocal(out=rinv[h][:], in_=denom[:])
-            pn.append(sb("pn%d" % h, [P, HALF_COLS]))
-            nc.gpsimd.tensor_tensor(out=teams(pn[h][:]), in0=teams(p[h][:]), in1=spread(rinv[h][:]), op=ALU.mult)
-
-        ta_ps = []
-        for h in range(HALVES):
+            a_ps.append(psum.tile([P, HALF_COLS], F32, name="a_ps%d" % h, tag="score", bufs=2))
+            products(a_ps[h], key_words[h], key_scales, h, query_mx)
             ta_ps.append(psum.tile([P, HALF_COLS], F32, name="ta_ps%d" % h))
             products(ta_ps[h], key_words[h], key_scales, h, dquery_mx)
-
-        gout_bf = round_and_interleave(gout_raw, "gout_bf")
-        base_sb = stage.tile([P, TILES, Q], F32, name="base_sb", tag="raw", align_bytes=64)
+            nc.scalar.activation(out=first[h][:, 0:TEAM, 0:HALF_TEAMS], in_=members(a_ps[h][:]), func=ACT.Exp)
+            nc.vector.tensor_tensor(out=first[h][:, 0:TEAM, HALF_TEAMS:], in0=members(ta_ps[h][:]), in1=first[h][:, 0:TEAM, 0:HALF_TEAMS], op=ALU.mult)
+        base_sb = staged("base_sb", [P, TILES, Q], F32, "c")
         nc.sync.dma_start(out=base_sb[:], in_=base.rearrange("(r p) q -> p r q", p=P))
-
-        tp, tsum = [], []
-        for h in range(HALVES):
-            tp.append(sb("tp%d" % h, [P, HALF_COLS]))
-            nc.vector.tensor_tensor(out=tp[h][:], in0=ta_ps[h][:], in1=p[h][:], op=ALU.mult)
-        for h in range(HALVES):
-            tsum.append(sb("tsum%d" % h, [P, HALF_TEAMS]))
-            nc.vector.tensor_reduce(out=tsum[h][:], in_=teams(tp[h][:]), axis=AXIS_X, op=ALU.add)
         val_words = [gather_words(val_pool, h, "val_words%d" % h) for h in range(HALVES)]
-        tmean, x, z = [], [], []
-        for h in range(HALVES):
-            tmean.append(sb("tmean%d" % h, [P, HALF_TEAMS]))
-            nc.vector.tensor_tensor(out=tmean[h][:], in0=tsum[h][:], in1=rinv[h][:], op=ALU.mult)
-        for h in range(HALVES):
-            f = sb("f%d" % h, [P, HALF_COLS])
-            nc.vector.tensor_tensor(out=teams(f[:]), in0=teams(ta_ps[h][:]), in1=spread(tmean[h][:]), op=ALU.subtract)
-            x.append(sb("x%d" % h, [P, HALF_COLS]))
-            nc.gpsimd.tensor_tensor(out=x[h][:], in0=f[:], in1=pn[h][:], op=ALU.mult)
-        gout_mx = quantize(gout_bf, "gout")
-        for h in range(HALVES):
-            rho = sb("rho%d" % h, [P, HALF_TEAMS])
-            nc.vector.tensor_tensor(out=by_tile(rho[:]), in0=by_tile(rinv[h][:]), in1=res_of(h), op=ALU.mult)
-            z.append(sb("z%d" % h, [P, HALF_TEAMS]))
-            nc.vector.tensor_tensor(out=z[h][:], in0=rho[:], in1=tmean[h][:], op=ALU.mult)
+
+        gout_mx = quantize(round_and_interleave(gout_raw, "gout_bf"), "gout")
+        late = staged("late", [P, 2 * HALF_COLS], F32, "b")
 
         c_ps = []
         for h in range(HALVES):
             c_ps.append(psum.tile([P, HALF_COLS], F32, name="c_ps%d" % h))
             products(c_ps[h], val_words[h], val_scales, h, gout_mx)
 
-        def c_of(r):
-            return c_ps[r // PER_HALF][:, Q * (r % PER_HALF) : Q * (r % PER_HALF + 1)]
-
-        def cols_of(tiles, r, width):
-            return tiles[r // PER_HALF][:, width * (r % PER_HALF) : width * (r % PER_HALF + 1)]
-
-        pc = [sb("pc%d" % h, [P, HALF_COLS]) for h in range(HALVES)]
-        m8 = [sb("m8_%d" % h, [P, HALF_TEAMS]) for h in range(HALVES)]
-        g8 = [sb("g8_%d" % r, [P, Q]) for r in range(TILES)]
-        y = [sb("y%d" % r, [P, Q]) for r in range(TILES)]
-        yb = [sb("yb%d" % r, [P, Q]) for r in range(TILES)]
-        mz = [sb("mz%d" % h, [P, HALF_TEAMS]) for h in range(HALVES)]
+        st = [team_sums(first[h], "st%d" % h, "turned", staged("st_sb%d" % h, [P, P], F32, "val_words%d" % h)[:]) for h in range(HALVES)]
         for h in range(HALVES):
-            for r in range(PER_HALF * h, PER_HALF * (h + 1)):
-                nc.vector.scalar_tensor_tensor(out=cols_of(pc, r, Q), in0=c_of(r), scalar=u8[:, r : r + 1], in1=cols_of(pn, r, Q), op0=ALU.mult, op1=ALU.mult)
-            nc.vector.tensor_reduce(out=m8[h][:], in_=teams(pc[h][:]), axis=AXIS_X, op=ALU.add)
+            p.append(late[:, HALF_COLS * h : HALF_COLS * (h + 1)])
+            nc.scalar.activation(out=p[h], in_=a_ps[h][:], func=ACT.Exp)
+
         for h in range(HALVES):
-            for r in range(PER_HALF * h, PER_HALF * (h + 1)):
-                nc.vector.scalar_tensor_tensor(out=teams(g8[r][:]), in0=teams(c_of(r)), scalar=u8[:, r : r + 1], in1=spread(cols_of(m8, r, G)), op0=ALU.mult, op1=ALU.subtract)
-                nc.gpsimd.tensor_tensor(out=y[r][:], in0=g8[r][:], in1=cols_of(x, r, Q), op=ALU.mult)
-            nc.vector.tensor_tensor(out=mz[h][:], in0=m8[h][:], in1=z[h][:], op=ALU.mult)
-        for r in range(TILES):
-            nc.gpsimd.tensor_tensor(out=yb[r][:], in0=y[r][:], in1=base_sb[:, r, :], op=ALU.add)
-        for r in range(TILES):
-            ysum = sb("ysum%d" % r, [P, G])
-            nc.vector.tensor_reduce(out=ysum[:], in_=teams(y[r][:]), axis=AXIS_X, op=ALU.add)
-            kappa = sb("kappa%d" % r, [P, G])
-            nc.vector.tensor_tensor(out=kappa[:], in0=ysum[:], in1=cols_of(mz, r, G), op=ALU.add)
-            kp = sb("kp%d" % r, [P, Q])
-            nc.vector.tensor_tensor(out=teams(kp[:]), in0=teams(cols_of(pn, r, Q)), in1=spread(kappa[:]), op=ALU.mult)
-            res_tile = sb("result%d" % r, [P, Q])
-            nc.vector.tensor_tensor(out=res_tile[:], in0=yb[r][:], in1=kp[:], op=ALU.subtract)
-            nc.sync.dma_start(out=out[P * r : P * (r + 1), :], in_=res_tile[:])
+            nc.vector.tensor_tensor(out=second[h][:, :, 0:HALF_TEAMS], in0=members(c_ps[h][:]), in1=first[h][:, 0:TEAM, 0:HALF_TEAMS], op=ALU.mult)
+            nc.vector.tensor_tensor(out=second[h][:, :, HALF_TEAMS:], in0=members(c_ps[h][:]), in1=first[h][:, 0:TEAM, HALF_TEAMS:], op=ALU.mult)
+        ab = [team_sums(second[h], "ab%d" % h, "score", sb("ab_sb%d" % h, [P, P])[:]) for h in range(HALVES)]
+
+        after = [held.tile([P, (TEAM + 1) * 2 * HALF_TEAMS], F32, name="after%d" % h, tag="first%d" % h, align_bytes=64) for h in range(HALVES)]
+        small0 = staged("small0", [P, 2 * HALF_TEAMS], F32, "a")
+        small = [small0[:], after[0][:, 2 * HALF_COLS :]]
+        rinv = [small[h][:, 0:HALF_TEAMS] for h in range(HALVES)]
+        tmean = [small[h][:, HALF_TEAMS:] for h in range(HALVES)]
+        pn = [after[h][:, 0:HALF_COLS] for h in range(HALVES)]
+        f = [after[h][:, HALF_COLS : 2 * HALF_COLS] for h in range(HALVES)]
+        for h in range(HALVES):
+            nc.vector.reciprocal(out=rinv[h], in_=st[h][:, 0:HALF_TEAMS])
+            nc.vector.tensor_tensor(out=tmean[h], in0=st[h][:, HALF_TEAMS:], in1=rinv[h], op=ALU.mult)
+            nc.vector.tensor_tensor(out=teams(pn[h]), in0=teams(p[h]), in1=spread(rinv[h]), op=ALU.mult)
+            nc.vector.tensor_tensor(out=teams(f[h]), in0=teams(ta_ps[h][:]), in1=spread(tmean[h]), op=ALU.subtract)
+
+        for h in range(HALVES):
+            means = sb("means%d" % h, [P, 2, HALF_TEAMS])
+            nc.vector.tensor_tensor(
+                out=means[:],
+                in0=ab[h].rearrange("p (k n) -> p k n", k=2),
+                in1=rinv[h].unsqueeze(1).to_broadcast([P, 2, HALF_TEAMS]),
+                op=ALU.mult,
+            )
+            tm = sb("tm%d" % h, [P, HALF_TEAMS])
+            nc.vector.tensor_tensor(out=tm[:], in0=means[:, 0, :], in1=tmean[h], op=ALU.mult)
+            kappa = sb("kappa%d" % h, [P, HALF_TEAMS])
+            nc.vector.tensor_tensor(out=kappa[:], in0=tm[:], in1=means[:, 1, :], op=ALU.subtract)
+            tiles = range(PER_HALF * h, PER_HALF * (h + 1))
+            work = {}
+            for r in tiles:
+                s = r % PER_HALF
+                work[r] = sb("g%d" % r, [P, Q])
+                nc.vector.tensor_tensor(out=teams(work[r][:]), in0=teams(c_ps[h][:, Q * s : Q * (s + 1)]), in1=spread(means[:, 0, G * s : G * (s + 1)]), op=ALU.subtract)
+            for r in tiles:
+                s = r % PER_HALF
+                nc.vector.tensor_tensor(out=work[r][:], in0=work[r][:], in1=f[h][:, Q * s : Q * (s + 1)], op=ALU.mult)
+            for r in tiles:
+                s = r % PER_HALF
+                nc.vector.tensor_tensor(out=teams(work[r][:]), in0=teams(work[r][:]), in1=spread(kappa[:, G * s : G * (s + 1)]), op=ALU.add)
+            for r in tiles:
+                s = r % PER_HALF
+                nc.vector.tensor_tensor(out=work[r][:], in0=work[r][:], in1=pn[h][:, Q * s : Q * (s + 1)], op=ALU.mult)
+            for r in tiles:
+                nc.vector.scalar_tensor_tensor(out=work[r][:], in0=work[r][:], scalar=u8[:, r : r + 1], in1=base_sb[:, r, :], op0=ALU.mult, op1=ALU.add)
+                nc.sync.dma_start(out=out[P * r : P * (r + 1), :], in_=work[r][:])

@@ -60,7 +60,7 @@ def tile_attend_hvteamshares_d_kernel(tc, query, keys_words, keys_scales, reserv
             return raw
 
         def round_and_interleave(raw, name, pieces=1):
-            grouped = sb(name, [P, Q, PACK], BF16)
+            grouped = staged(name, [P, Q, PACK], BF16, name)
             width = Q // pieces
             for piece in range(pieces):
                 cols = slice(width * piece, width * (piece + 1))
@@ -94,7 +94,7 @@ def tile_attend_hvteamshares_d_kernel(tc, query, keys_words, keys_scales, reserv
         offsets = held.tile([P, I // 16], U16, name="offsets")
         key_scale_pool = sb("key_scale_pool", [P, T], U8)
         val_scale_pool = sb("val_scale_pool", [P, T], U8)
-        key_pool = staged("key_pool", [P, T], I32, "c")
+        key_pool = sb("key_pool", [P, T], I32)
 
         nc.gpsimd.memset(key_scale_pool[:].bitcast(I32), 0)
         nc.vector.memset(val_scale_pool[:].bitcast(I32), 0)
@@ -104,20 +104,18 @@ def tile_attend_hvteamshares_d_kernel(tc, query, keys_words, keys_scales, reserv
         query_raw = load_rows(query, "query_raw", "a")
         dquery_raw = load_rows(dquery, "dquery_raw", "b")
         nc.sync.dma_start(out=key_pool[:], in_=keys_words[0].rearrange("p n t -> p (n t)").bitcast(I32))
-        for quadrant in range(4):
-            load_scale_rows(nc.sync, val_scale_pool, vals_scales, quadrant)
-
         slot_rows = sb("slot_rows", [P, P])
         identity = sb("identity", [P, P])
         nc.gpsimd.memset(slot_rows[:], 0.0)
-        nc.gpsimd.dma_start(out=slot_rows[0:TILES, :], in_=reserve.rearrange("(r p) o -> r (p o)", p=P))
-        nc.gpsimd.dma_start(out=slot_rows[TILES : 2 * TILES, :], in_=us.rearrange("(r p) o -> r (p o)", p=P))
+        nc.sync.dma_start(out=slot_rows[0:TILES, :], in_=reserve.rearrange("(r p) o -> r (p o)", p=P))
+        nc.sync.dma_start(out=slot_rows[TILES : 2 * TILES, :], in_=us.rearrange("(r p) o -> r (p o)", p=P))
         make_identity(nc, identity[:])
 
-        first = [held.tile([P, TEAM + 1, 2 * HALF_TEAMS], F32, name="first%d" % h, tag="first%d" % h, align_bytes=64) for h in range(HALVES)]
+        for quadrant in range(4):
+            load_scale_rows(nc.sync, val_scale_pool, vals_scales, quadrant)
+
+        first = [held.tile([P, TEAM, 2 * HALF_TEAMS], F32, name="first%d" % h, tag="first%d" % h, align_bytes=64) for h in range(HALVES)]
         second = [sb("second%d" % h, [P, TEAM, 2 * HALF_TEAMS]) for h in range(HALVES)]
-        for h in range(HALVES):
-            nc.gpsimd.memset(first[h][:, TEAM, HALF_TEAMS:], 0.0)
 
         slot_cols_ps = psum.tile([P, P], F32, name="slot_cols_ps", tag="turned", bufs=2)
         nc.tensor.transpose(slot_cols_ps[:], slot_rows[:], identity[:])
@@ -133,12 +131,17 @@ def tile_attend_hvteamshares_d_kernel(tc, query, keys_words, keys_scales, reserv
 
         u8 = sb("u8", [P, TILES])
         nc.scalar.activation(out=u8[:], in_=slot_cols_ps[:, TILES : 2 * TILES], func=ACT.Copy, scale=OUT_FACTOR)
-        for h in range(HALVES):
+
+        def reserve_row(h, row):
+            pairs = slot_cols_ps[:, 0 : 4 * TILES].rearrange("p (k r) -> p k r", k=2)[:, :, PER_HALF * h : PER_HALF * (h + 1)]
             nc.scalar.activation(
-                out=first[h][:, TEAM, 0:HALF_TEAMS].rearrange("p (s g) -> p s g", g=G),
-                in_=slot_cols_ps[:, PER_HALF * h : PER_HALF * (h + 1)].unsqueeze(2).to_broadcast([P, PER_HALF, G]),
+                out=row.rearrange("p (k s g) -> p k s g", k=2, g=G),
+                in_=pairs.unsqueeze(3).to_broadcast([P, 2, PER_HALF, G]),
                 func=ACT.Copy,
             )
+            return row
+
+        reserve_rows = [reserve_row(0, sb("reserve_row0", [P, P])[:])]
 
         def gather_words(pool_tile, h, name):
             words = staged(name, [P, HALF_SLOTS], U32, name)
@@ -149,12 +152,13 @@ def tile_attend_hvteamshares_d_kernel(tc, query, keys_words, keys_scales, reserv
         def members(ap):
             return ap.rearrange("p (n j) -> p j n", j=TEAM)
 
-        def team_sums(rows, name, tag, turned_sb):
+        def team_sums(rows, name, tag, copy_tag):
             bank = psum.tile([P, 2, P], F32, name=name + "_bank", tag=tag, bufs=2)
             turned, sums = bank[:, 0, :], bank[:, 1, :]
-            count = rows.shape[1]
+            count = len(rows)
             for j in range(count):
-                nc.tensor.matmul(turned, lhsT=rows[:, j, :], rhs=identity[:], start=(j == 0), stop=(j == count - 1), is_transpose=True)
+                nc.tensor.matmul(turned, lhsT=rows[j], rhs=identity[:], start=(j == 0), stop=(j == count - 1), is_transpose=True)
+            turned_sb = staged(name + "_sb", [P, P], F32, copy_tag)[:]
             nc.scalar.copy(out=turned_sb, in_=turned)
             nc.tensor.transpose(sums, turned_sb, identity[:])
             return sums
@@ -169,13 +173,13 @@ def tile_attend_hvteamshares_d_kernel(tc, query, keys_words, keys_scales, reserv
             products(a_ps[h], key_words[h], key_scales, h, query_mx)
             ta_ps.append(psum.tile([P, HALF_COLS], F32, name="ta_ps%d" % h))
             products(ta_ps[h], key_words[h], key_scales, h, dquery_mx)
-            nc.scalar.activation(out=first[h][:, 0:TEAM, 0:HALF_TEAMS], in_=members(a_ps[h][:]), func=ACT.Exp)
-            nc.vector.tensor_tensor(out=first[h][:, 0:TEAM, HALF_TEAMS:], in0=members(ta_ps[h][:]), in1=first[h][:, 0:TEAM, 0:HALF_TEAMS], op=ALU.mult)
-        base_sb = staged("base_sb", [P, TILES, Q], F32, "c")
-        nc.sync.dma_start(out=base_sb[:], in_=base.rearrange("(r p) q -> p r q", p=P))
+            nc.scalar.activation(out=first[h][:, :, 0:HALF_TEAMS], in_=members(a_ps[h][:]), func=ACT.Exp)
+            nc.vector.tensor_tensor(out=first[h][:, :, HALF_TEAMS:], in0=members(ta_ps[h][:]), in1=first[h][:, :, 0:HALF_TEAMS], op=ALU.mult)
         val_words = [gather_words(val_pool, h, "val_words%d" % h) for h in range(HALVES)]
 
         gout_mx = quantize(round_and_interleave(gout_raw, "gout_bf"), "gout")
+        base_sb = staged("base_sb", [P, TILES, Q], F32, "gout_bf")
+        nc.sync.dma_start(out=base_sb[:], in_=base.rearrange("(r p) q -> p r q", p=P))
         late = staged("late", [P, 2 * HALF_COLS], F32, "b")
 
         c_ps = []
@@ -183,15 +187,16 @@ def tile_attend_hvteamshares_d_kernel(tc, query, keys_words, keys_scales, reserv
             c_ps.append(psum.tile([P, HALF_COLS], F32, name="c_ps%d" % h))
             products(c_ps[h], val_words[h], val_scales, h, gout_mx)
 
-        st = [team_sums(first[h], "st%d" % h, "turned", staged("st_sb%d" % h, [P, P], F32, "val_words%d" % h)[:]) for h in range(HALVES)]
+        reserve_rows.append(reserve_row(1, staged("reserve_row1", [P, P], F32, "val_words1")[:]))
+        st = [team_sums([first[h][:, j, :] for j in range(TEAM)] + [reserve_rows[h]], "st%d" % h, "turned", "val_words%d" % h) for h in range(HALVES)]
         for h in range(HALVES):
             p.append(late[:, HALF_COLS * h : HALF_COLS * (h + 1)])
             nc.scalar.activation(out=p[h], in_=a_ps[h][:], func=ACT.Exp)
 
         for h in range(HALVES):
-            nc.vector.tensor_tensor(out=second[h][:, :, 0:HALF_TEAMS], in0=members(c_ps[h][:]), in1=first[h][:, 0:TEAM, 0:HALF_TEAMS], op=ALU.mult)
-            nc.vector.tensor_tensor(out=second[h][:, :, HALF_TEAMS:], in0=members(c_ps[h][:]), in1=first[h][:, 0:TEAM, HALF_TEAMS:], op=ALU.mult)
-        ab = [team_sums(second[h], "ab%d" % h, "score", sb("ab_sb%d" % h, [P, P])[:]) for h in range(HALVES)]
+            nc.vector.tensor_tensor(out=second[h][:, :, 0:HALF_TEAMS], in0=members(c_ps[h][:]), in1=first[h][:, :, 0:HALF_TEAMS], op=ALU.mult)
+            nc.vector.tensor_tensor(out=second[h][:, :, HALF_TEAMS:], in0=members(c_ps[h][:]), in1=first[h][:, :, HALF_TEAMS:], op=ALU.mult)
+        ab = [team_sums([second[h][:, j, :] for j in range(TEAM)], "ab%d" % h, "score", "ab_sb%d" % h) for h in range(HALVES)]
 
         after = [held.tile([P, (TEAM + 1) * 2 * HALF_TEAMS], F32, name="after%d" % h, tag="first%d" % h, align_bytes=64) for h in range(HALVES)]
         small0 = staged("small0", [P, 2 * HALF_TEAMS], F32, "a")

from contextlib import ExitStack

import concourse.mybir as mybir
from concourse.masks import make_identity

D, E, T, I, Q, G = 512, 512, 2048, 512, 256, 32
FLOPS = 2 * I * Q * (D + D + E)

F32 = mybir.dt.float32
BF16 = mybir.dt.bfloat16
I32 = mybir.dt.int32
U32 = mybir.dt.uint32
U16 = mybir.dt.uint16
U8 = mybir.dt.uint8
FP8X4 = mybir.dt.float8_e4m3fn_x4
ALU = mybir.AluOpType
ACT = mybir.ActivationFunctionType
AXIS_X = mybir.AxisListType.X

P = 128
PACK = 4
TEAM = Q // G
TILES = I // P
HALVES = 2
PER_HALF = TILES // HALVES
HALF_SLOTS = I // HALVES
HALF_COLS = PER_HALF * Q
HALF_TEAMS = PER_HALF * G
OUT_FACTOR = 8.0


def tile_attend_hvteamshares_d_kernel(tc, query, keys_words, keys_scales, reserve, us, gout, vals_words, vals_scales, dquery, base, offs, out):
    nc = tc.nc
    with ExitStack() as ctx:
        held = ctx.enter_context(tc.tile_pool(name="held", bufs=1))
        stage = ctx.enter_context(tc.tile_pool(name="stage", bufs=1))
        psum = ctx.enter_context(tc.psum_pool(name="psum", bufs=1))

        def sb(name, shape, dtype=F32):
            return held.tile(shape, dtype, name=name, align_bytes=64)

        def teams(ap):
            return ap.rearrange("p (n j) -> p n j", j=TEAM)

        def spread(ap):
            return ap.unsqueeze(2).to_broadcast([P, ap.shape[1], TEAM])

        def load_scale_rows(queue, window, scales, quadrant):
            queue.dma_start(
                out=window[32 * quadrant : 32 * quadrant + 4, :].bitcast(I32),
                in_=scales[0, 4 * quadrant : 4 * quadrant + 4, :].bitcast(I32),
            )

        def staged(name, shape, dtype, tag):
            return stage.tile(shape, dtype, name=name, tag=tag, align_bytes=64)

        def load_rows(src, name, tag):
            raw = staged(name, [P, PACK, Q], F32, tag)
            nc.sync.dma_start(out=raw[:], in_=src.rearrange("(p t) q -> p t q", t=PACK))
            return raw

        def round_and_interleave(raw, name, pieces=1):
            grouped = staged(name, [P, Q, PACK], BF16, name)
            width = Q // pieces
            for piece in range(pieces):
                cols = slice(width * piece, width * (piece + 1))
                nc.scalar.activation(
                    out=grouped[:, cols, :].rearrange("p (c i) t -> p c t i", i=4),
                    in_=raw[:, :, cols].rearrange("p t (c i) -> p c t i", i=4),
                    func=ACT.Copy,
                )
            return grouped

        def quantize(grouped, name):
            codes = sb(name + "_codes", [P, Q], U32)
            plane = sb(name + "_plane", [P, Q], U8)
            nc.vector.quantize_mx(out=codes[:].bitcast(FP8X4), scales=plane[:], in_=grouped[:].rearrange("p q t -> p (q t)"))
            return codes, plane

        def products(bank, words, scale_bytes, h, moving):
            codes, plane = moving
            for s in range(PER_HALF):
                slot0 = HALF_SLOTS * h + P * s
                nc.tensor.matmul_mx(
                    out=bank[:, Q * s : Q * (s + 1)],
                    lhsT=words[:, P * s : P * (s + 1)].bitcast(FP8X4),
                    lhsT_scale=scale_bytes[:, slot0 : slot0 + P],
                    rhs=codes[:].bitcast(FP8X4),
                    rhs_scale=plane[:],
                    start=True,
                    stop=True,
                )

        offsets = held.tile([P, I // 16], U16, name="offsets")
        key_scale_pool = sb("key_scale_pool", [P, T], U8)
        val_scale_pool = sb("val_scale_pool", [P, T], U8)
        key_pool = sb("key_pool", [P, T], I32)

        nc.gpsimd.memset(key_scale_pool[:].bitcast(I32), 0)
        nc.vector.memset(val_scale_pool[:].bitcast(I32), 0)
        for quadrant in range(4):
            load_scale_rows(nc.sync, key_scale_pool, keys_scales, quadrant)
        nc.sync.dma_start(offsets[:], offs)
        query_raw = load_rows(query, "query_raw", "a")
        dquery_raw = load_rows(dquery, "dquery_raw", "b")
        nc.sync.dma_start(out=key_pool[:], in_=keys_words[0].rearrange("p n t -> p (n t)").bitcast(I32))
        slot_rows = sb("slot_rows", [P, P])
        identity = sb("identity", [P, P])
        nc.gpsimd.memset(slot_rows[:], 0.0)
        nc.sync.dma_start(out=slot_rows[0:TILES, :], in_=reserve.rearrange("(r p) o -> r (p o)", p=P))
        nc.sync.dma_start(out=slot_rows[TILES : 2 * TILES, :], in_=us.rearrange("(r p) o -> r (p o)", p=P))
        make_identity(nc, identity[:])

        for quadrant in range(4):
            load_scale_rows(nc.sync, val_scale_pool, vals_scales, quadrant)

        first = [held.tile([P, TEAM, 2 * HALF_TEAMS], F32, name="first%d" % h, tag="first%d" % h, align_bytes=64) for h in range(HALVES)]
        second = [sb("second%d" % h, [P, TEAM, 2 * HALF_TEAMS]) for h in range(HALVES)]

        slot_cols_ps = psum.tile([P, P], F32, name="slot_cols_ps", tag="turned", bufs=2)
        nc.tensor.transpose(slot_cols_ps[:], slot_rows[:], identity[:])

        key_scales = sb("key_scales", [P, I], U8)
        nc.vector.tensor_copy(key_scales[:], key_scale_pool[:].indirect(offsets[:]))
        query_mx = quantize(round_and_interleave(query_raw, "query_bf"), "query")
        dquery_mx = quantize(round_and_interleave(dquery_raw, "dquery_bf"), "dquery")
        val_pool = staged("val_pool", [P, T], I32, "a")
        nc.sync.dma_start(out=val_pool[:], in_=vals_words[0].rearrange("p n t -> p (n t)").bitcast(I32))

        gout_raw = load_rows(gout, "gout_raw", "b")

        u8 = sb("u8", [P, TILES])
        nc.scalar.activation(out=u8[:], in_=slot_cols_ps[:, TILES : 2 * TILES], func=ACT.Copy, scale=OUT_FACTOR)

        def reserve_row(h, row):
            pairs = slot_cols_ps[:, 0 : 4 * TILES].rearrange("p (k r) -> p k r", k=2)[:, :, PER_HALF * h : PER_HALF * (h + 1)]
            nc.scalar.activation(
                out=row.rearrange("p (k s g) -> p k s g", k=2, g=G),
                in_=pairs.unsqueeze(3).to_broadcast([P, 2, PER_HALF, G]),
                func=ACT.Copy,
            )
            return row

        reserve_rows = [reserve_row(0, sb("reserve_row0", [P, P])[:])]

        def gather_words(pool_tile, h, name):
            words = staged(name, [P, HALF_SLOTS], U32, name)
            cols = HALF_SLOTS // 16
            nc.vector.tensor_copy(words[:], pool_tile[:].bitcast(U32).indirect(offsets[:, cols * h : cols * (h + 1)]))
            return words

        def members(ap):
            return ap.rearrange("p (n j) -> p j n", j=TEAM)

        def team_sums(rows, name, tag, copy_tag):
            bank = psum.tile([P, 2, P], F32, name=name + "_bank", tag=tag, bufs=2)
            turned, sums = bank[:, 0, :], bank[:, 1, :]
            count = len(rows)
            for j in range(count):
                nc.tensor.matmul(turned, lhsT=rows[j], rhs=identity[:], start=(j == 0), stop=(j == count - 1), is_transpose=True)
            turned_sb = staged(name + "_sb", [P, P], F32, copy_tag)[:]
            nc.scalar.copy(out=turned_sb, in_=turned)
            nc.tensor.transpose(sums, turned_sb, identity[:])
            return sums

        key_words = [gather_words(key_pool, h, "key_words%d" % h) for h in range(HALVES)]
        val_scales = sb("val_scales", [P, I], U8)
        nc.vector.tensor_copy(val_scales[:], val_scale_pool[:].indirect(offsets[:]))

        a_ps, ta_ps, p = [], [], []
        for h in range(HALVES):
            a_ps.append(psum.tile([P, HALF_COLS], F32, name="a_ps%d" % h, tag="score", bufs=2))
            products(a_ps[h], key_words[h], key_scales, h, query_mx)
            ta_ps.append(psum.tile([P, HALF_COLS], F32, name="ta_ps%d" % h))
            products(ta_ps[h], key_words[h], key_scales, h, dquery_mx)
            nc.scalar.activation(out=first[h][:, :, 0:HALF_TEAMS], in_=members(a_ps[h][:]), func=ACT.Exp)
            nc.vector.tensor_tensor(out=first[h][:, :, HALF_TEAMS:], in0=members(ta_ps[h][:]), in1=first[h][:, :, 0:HALF_TEAMS], op=ALU.mult)
        val_words = [gather_words(val_pool, h, "val_words%d" % h) for h in range(HALVES)]

        gout_mx = quantize(round_and_interleave(gout_raw, "gout_bf"), "gout")
        base_sb = staged("base_sb", [P, TILES, Q], F32, "gout_bf")
        nc.sync.dma_start(out=base_sb[:], in_=base.rearrange("(r p) q -> p r q", p=P))
        late = staged("late", [P, 2 * HALF_COLS], F32, "b")

        c_ps = []
        for h in range(HALVES):
            c_ps.append(psum.tile([P, HALF_COLS], F32, name="c_ps%d" % h))
            products(c_ps[h], val_words[h], val_scales, h, gout_mx)

        reserve_rows.append(reserve_row(1, staged("reserve_row1", [P, P], F32, "val_words1")[:]))
        st = [team_sums([first[h][:, j, :] for j in range(TEAM)] + [reserve_rows[h]], "st%d" % h, "turned", "val_words%d" % h) for h in range(HALVES)]
        for h in range(HALVES):
            p.append(late[:, HALF_COLS * h : HALF_COLS * (h + 1)])
            nc.scalar.activation(out=p[h], in_=a_ps[h][:], func=ACT.Exp)

        for h in range(HALVES):
            nc.vector.tensor_tensor(out=second[h][:, :, 0:HALF_TEAMS], in0=members(c_ps[h][:]), in1=first[h][:, :, 0:HALF_TEAMS], op=ALU.mult)
            nc.vector.tensor_tensor(out=second[h][:, :, HALF_TEAMS:], in0=members(c_ps[h][:]), in1=first[h][:, :, HALF_TEAMS:], op=ALU.mult)
        ab = [team_sums([second[h][:, j, :] for j in range(TEAM)], "ab%d" % h, "score", "ab_sb%d" % h) for h in range(HALVES)]

        after = [held.tile([P, (TEAM + 1) * 2 * HALF_TEAMS], F32, name="after%d" % h, tag="first%d" % h, align_bytes=64) for h in range(HALVES)]
        small0 = staged("small0", [P, 2 * HALF_TEAMS], F32, "a")
        small = [small0[:], after[0][:, 2 * HALF_COLS :]]
        rinv = [small[h][:, 0:HALF_TEAMS] for h in range(HALVES)]
        tmean = [small[h][:, HALF_TEAMS:] for h in range(HALVES)]
        pn = [after[h][:, 0:HALF_COLS] for h in range(HALVES)]
        f = [after[h][:, HALF_COLS : 2 * HALF_COLS] for h in range(HALVES)]
        for h in range(HALVES):
            nc.vector.reciprocal(out=rinv[h], in_=st[h][:, 0:HALF_TEAMS])
            nc.vector.tensor_tensor(out=tmean[h], in0=st[h][:, HALF_TEAMS:], in1=rinv[h], op=ALU.mult)
            nc.vector.tensor_tensor(out=teams(pn[h]), in0=teams(p[h]), in1=spread(rinv[h]), op=ALU.mult)
            nc.vector.tensor_tensor(out=teams(f[h]), in0=teams(ta_ps[h][:]), in1=spread(tmean[h]), op=ALU.subtract)

        for h in range(HALVES):
            means = sb("means%d" % h, [P, 2, HALF_TEAMS])
            nc.vector.tensor_tensor(
                out=means[:],
                in0=ab[h].rearrange("p (k n) -> p k n", k=2),
                in1=rinv[h].unsqueeze(1).to_broadcast([P, 2, HALF_TEAMS]),
                op=ALU.mult,
            )
            tm = sb("tm%d" % h, [P, HALF_TEAMS])
            nc.vector.tensor_tensor(out=tm[:], in0=means[:, 0, :], in1=tmean[h], op=ALU.mult)
            kappa = sb("kappa%d" % h, [P, HALF_TEAMS])
            nc.vector.tensor_tensor(out=kappa[:], in0=tm[:], in1=means[:, 1, :], op=ALU.subtract)
            tiles = range(PER_HALF * h, PER_HALF * (h + 1))
            work = {}
            for r in tiles:
                s = r % PER_HALF
                work[r] = sb("g%d" % r, [P, Q])
                nc.vector.tensor_tensor(out=teams(work[r][:]), in0=teams(c_ps[h][:, Q * s : Q * (s + 1)]), in1=spread(means[:, 0, G * s : G * (s + 1)]), op=ALU.subtract)
            for r in tiles:
                s = r % PER_HALF
                nc.vector.tensor_tensor(out=work[r][:], in0=work[r][:], in1=f[h][:, Q * s : Q * (s + 1)], op=ALU.mult)
            for r in tiles:
                s = r % PER_HALF
                nc.vector.tensor_tensor(out=teams(work[r][:]), in0=teams(work[r][:]), in1=spread(kappa[:, G * s : G * (s + 1)]), op=ALU.add)
            for r in tiles:
                s = r % PER_HALF
                nc.vector.tensor_tensor(out=work[r][:], in0=work[r][:], in1=pn[h][:, Q * s : Q * (s + 1)], op=ALU.mult)
            for r in tiles:
                nc.vector.scalar_tensor_tensor(out=work[r][:], in0=work[r][:], scalar=u8[:, r : r + 1], in1=base_sb[:, r, :], op0=ALU.mult, op1=ALU.add)
                nc.sync.dma_start(out=out[P * r : P * (r + 1), :], in_=work[r][:])
